import numpy as np
import ml_dtypes


def mxq(x, axis, fmt="e4m3"):
    dtype, down = {"e4m3": (ml_dtypes.float8_e4m3fn, 7), "e5m2": (ml_dtypes.float8_e5m2, 14)}[fmt]
    v = np.moveaxis(np.asarray(x, np.float32).astype(ml_dtypes.bfloat16).astype(np.float64), axis, -1)
    blocks = v.reshape(v.shape[:-1] + (-1, 32))
    amax = np.abs(blocks).max(-1, keepdims=True)
    byte = np.maximum(np.where(amax > 0, np.frexp(amax)[1] - 1 + 127, 0) - down, 1)
    scale = np.exp2(byte - 127.0)
    codes = (blocks / scale).astype(np.float32).astype(dtype).astype(np.float64)
    return np.moveaxis((codes * scale).reshape(v.shape), -1, axis)


WIDE = False


def mx_kscale(k):
    if not WIDE:
        return np.ones(k)
    levels = np.array([10, -10, 5, -5, 0])
    if k % 512:
        return np.exp2(np.random.permutation(np.resize(levels, k // 32))).repeat(32)
    a = np.empty((k // 512, 16))
    for p in range(k // 512):
        a[p, :8] = np.random.permutation(np.resize(levels, 8))
        for g in range(8):
            far = levels[np.abs(levels - a[p, g]) >= 10]
            a[p, g + 8] = far[np.random.randint(len(far))]
    return np.exp2(a.ravel()).repeat(32)


def f64(x):
    return np.asarray(x).astype(np.float64)


def striped(idx):
    return np.tile(np.asarray(idx).reshape(-1, 16).T, (8, 1)).astype(np.uint16)


def unstriped(offs):
    return offs[:16].T.reshape(-1).astype(np.int64)


def striped8(idx):
    return np.asarray(idx).reshape(8, -1, 16).transpose(0, 2, 1).reshape(128, -1).astype(np.uint16)


def unstriped8(offs):
    return offs.reshape(8, 16, -1).transpose(0, 2, 1).reshape(8, -1).astype(np.int64)


def pick8(x, idx, run):
    r = np.arange(len(x))
    return x[r[:, None], idx[r % (8 * run) // run]]


E2M1 = np.array([0.0, 0.5, 1.0, 1.5, 2.0, 3.0, 4.0, 6.0, -0.0, -0.5, -1.0, -1.5, -2.0, -3.0, -4.0, -6.0])


def pack_weight(w, fmt):
    k, n = w.shape
    w = f64(np.asarray(w, np.float32).astype(ml_dtypes.bfloat16)).reshape(k // 32, 32, n)
    amax = np.abs(w).max(1)
    if fmt == "e4m3":
        byte = np.frexp(amax)[1] - 1 + 127 - 7
    else:
        mant, ex = np.frexp(amax / 6.0)
        byte = np.where(mant > 0.5, ex, ex - 1) + 127
    byte = np.clip(np.where(amax > 0, byte, 1), 1, 254)
    scaled = (w * np.exp2(127.0 - byte)[:, None, :]).reshape(k, n).astype(np.float32)
    by_word = np.ascontiguousarray(scaled.reshape(k // 512, 128, 4, n).transpose(0, 1, 3, 2))
    if fmt == "e4m3":
        words = by_word.astype(ml_dtypes.float8_e4m3fn).view(np.uint8)
    else:
        c = by_word.astype(ml_dtypes.float4_e2m1fn).view(np.uint8) & 0xF
        words = (c[..., 0::2] | (c[..., 1::2] << 4)).reshape(k // 512, 128, 2 * n)
    return np.ascontiguousarray(words), np.ascontiguousarray(byte.astype(np.uint8).reshape(k // 512, 16, n))


def unpack_weight(words, scales, fmt):
    g, _, n = scales.shape
    words = np.ascontiguousarray(words).reshape(g, 128, n, -1)
    if fmt == "e4m3":
        vals = words.view(ml_dtypes.float8_e4m3fn).astype(np.float64)
    else:
        nib = np.empty((g, 128, n, 4), np.uint8)
        nib[..., 0::2] = words & 0xF
        nib[..., 1::2] = words >> 4
        vals = E2M1[nib]
    vals = vals * np.repeat(np.exp2(scales.astype(np.float64) - 127.0), 8, axis=1)[..., None]
    return vals.transpose(0, 1, 3, 2).reshape(g * 512, n)


K, J, R, T, F, G, O, S, N = 512, 512, 512, 1024, 1024, 1024, 128, 256, 256


def setup_inputs():
    n = np.random.standard_normal
    idx = np.random.permutation(T)[:J]
    idx2 = np.stack([np.random.permutation(F)[:R] for _ in range(8)])
    idx3 = np.stack([np.random.permutation(G)[:R] for _ in range(8)])
    idx4 = np.stack([np.random.permutation(J)[:S] for _ in range(8)])
    idx5 = np.stack([np.random.permutation(S)[:O] for _ in range(8)])
    idx6 = np.random.permutation(S)[:O]
    idx7 = np.random.permutation(T)[:O]
    fk = mx_kscale(K)
    fr = mx_kscale(R)
    xtp = pack_weight(n((K, T)) * fk[:, None], "e2m1")
    wbp = pack_weight(n((R, N)) * 1 / np.sqrt(R) / fr[:, None], "e4m3")
    wsp = pack_weight(n((K, N)) * 1 / np.sqrt(K) / fk[:, None], "e4m3")
    return {
        "xt_words": xtp[0],
        "xt_scales": xtp[1],
        "ua": (np.random.randint(-7, 8, (K, F)).astype(np.float64)).astype(np.float32),
        "ub": (np.random.randint(-7, 8, (K, G)).astype(np.float64)).astype(np.float32),
        "ha": ((np.random.randint(8, 25, (K, 1)) / 1024.0) / fk[:, None]).astype(np.float32),
        "hb": ((np.random.randint(8, 25, (K, 1)) / 1024.0) / fk[:, None]).astype(np.float32),
        "sa": (np.random.uniform(0.5, 1.6, (R, 1)) * fr[:, None]).astype(np.float32),
        "sb": (np.random.uniform(0.5, 1.6, (R, 1))).astype(np.float32),
        "sd": (np.random.uniform(0.5, 1.6, (R, 1))).astype(np.float32),
        "wb_words": wbp[0],
        "wb_scales": wbp[1],
        "ws_words": wsp[0],
        "ws_scales": wsp[1],
        "offs": striped(idx),
        "offs2": striped8(idx2),
        "offs3": striped8(idx3),
        "offs4": striped8(idx4),
        "offs5": striped8(idx5),
        "offs6": striped(idx6),
        "offs7": striped(idx7),
    }


def reference(xt_words, xt_scales, ua, ub, ha, hb, sa, sb, sd, wb_words, wb_scales, ws_words, ws_scales, offs, offs2, offs3, offs4, offs5, offs6, offs7):
    idx = unstriped(offs)
    idx2 = unstriped8(offs2)
    idx3 = unstriped8(offs3)
    idx4 = unstriped8(offs4)
    idx5 = unstriped8(offs5)
    idx6 = unstriped(offs6)
    idx7 = unstriped(offs7)
    xtu = unpack_weight(xt_words, xt_scales, "e2m1")
    wbu = unpack_weight(wb_words, wb_scales, "e4m3")
    wsu = unpack_weight(ws_words, ws_scales, "e4m3")
    wc = np.maximum(pick8(f64(ua), idx2, 64) * f64(ha), pick8(f64(ub), idx3, 64) * f64(hb))
    wcq = mxq(wc, 0, "e4m3")
    xtidxg = xtu[:, idx]
    a = wcq.T @ xtidxg
    h1 = pick8(a, idx4, 64) * f64(sa)
    hid = np.maximum(pick8(h1, idx5, 64) * f64(sb), h1[:, idx6] * f64(sd))
    hidq = mxq(hid, 0, "e4m3")
    xtidx7g = xtu[:, idx7]
    y = wbu.T @ hidq + wsu.T @ xtidx7g
    return y

@@ -1,0 +1,251 @@
+from contextlib import ExitStack
+
+import concourse.mybir as mybir
+
+K, J, R, T, F, G, O, S, N = 512, 512, 512, 1024, 1024, 1024, 128, 256, 256
+FLOPS = 2 * K * R * J + 2 * R * N * O + 2 * K * N * O
+
+F32 = mybir.dt.float32
+BF16 = mybir.dt.bfloat16
+I32 = mybir.dt.int32
+U32 = mybir.dt.uint32
+U16 = mybir.dt.uint16
+U8 = mybir.dt.uint8
+FP8X4 = mybir.dt.float8_e4m3fn_x4
+FP4X4 = mybir.dt.float4_e2m1fn_x4
+COPY = mybir.ActivationFunctionType.Copy
+MAX = mybir.AluOpType.max
+
+P = 128
+PACK = 4
+PER_COLUMN = 16
+
+
+def tile_picked_tokens_largercode_one_chain_further_plain_kernel(
+    tc, xt_words, xt_scales, ua, ub, ha, hb, sa, sb, sd, wb_words, wb_scales, ws_words, ws_scales,
+    offs, offs2, offs3, offs4, offs5, offs6, offs7, out,
+):
+    nc = tc.nc
+    with ExitStack() as ctx:
+        keep = ctx.enter_context(tc.tile_pool(name="keep", bufs=1))
+        psum = ctx.enter_context(tc.psum_pool(name="psum", bufs=1))
+
+        def tile(name, columns, dtype, tag=None):
+            return keep.tile([P, columns], dtype, name=name, tag=tag or name, align_bytes=64)
+
+        def load_list(name, source):
+            held = tile(name, source.shape[1], U16)
+            nc.sync.dma_start(held[:], source)
+            return held
+
+        def load_factor(queue, name, source):
+            held = tile(name, PACK, F32)
+            queue.dma_start(out=held[:], in_=source.rearrange("(p t) one -> p (t one)", t=PACK))
+            return held
+
+        def load_plane(name, table, t):
+            held = tile(name, table.shape[1], F32)
+            nc.sync.dma_start(out=held[:], in_=table.rearrange("(p t) f -> p t f", t=PACK)[:, t, :])
+            return held
+
+        def zeroed_scales(name, columns):
+            held = tile(name, columns, U8)
+            nc.vector.memset(held[:].bitcast(I32), 0)
+            return held
+
+        def load_scales(queue, held, source):
+            for row in range(PACK):
+                queue.dma_start(out=held[row:P:32, :].bitcast(I32), in_=source[0, row:16:PACK, :].bitcast(I32))
+
+        def load_words(name, source):
+            held = tile(name, N, U32)
+            nc.sync.dma_start(out=held[:].bitcast(I32), in_=source[0].rearrange("p n t -> p (n t)").bitcast(I32))
+            return held
+
+        def fetch(dst, window, offsets, factor, t):
+            nc.scalar.activation(out=dst, in_=window[:].indirect(offsets), func=COPY, scale=factor[:, t:t + 1])
+
+        x_scales = zeroed_scales("x_scales", T)
+        ws_sc = zeroed_scales("ws_sc", N)
+        wb_sc = zeroed_scales("wb_sc", N)
+        sa_t = load_factor(nc.gpsimd, "sa_t", sa)
+        sb_t = load_factor(nc.gpsimd, "sb_t", sb)
+        sd_t = load_factor(nc.gpsimd, "sd_t", sd)
+
+        ua_t = [load_plane("ua0", ua, 0)]
+        l2 = load_list("l2", offs2)
+        ha_t = load_factor(nc.sync, "ha_t", ha)
+        ub_t = [load_plane("ub0", ub, 0)]
+        l3 = load_list("l3", offs3)
+        hb_t = load_factor(nc.sync, "hb_t", hb)
+        l1 = load_list("l1", offs)
+        ua_t.append(load_plane("ua1", ua, 1))
+        x_stage = keep.tile([P, 2, T], U8, name="x_stage", align_bytes=64)
+        for h in range(2):
+            nc.sync.dma_start(
+                out=x_stage[64 * h:64 * h + PACK].bitcast(I32),
+                in_=xt_scales[0, 8 * h:8 * h + 8, :].rearrange("(q j) c -> j q c", j=PACK).bitcast(I32),
+            )
+        l7 = load_list("l7", offs7)
+        ub_t.append(load_plane("ub1", ub, 1))
+        ua_t.append(load_plane("ua2", ua, 2))
+        x_words = tile("x_words", T, U16)
+        nc.sync.dma_start(out=x_words[:].bitcast(I32), in_=xt_words[0].bitcast(I32))
+        ub_t.append(load_plane("ub2", ub, 2))
+        ua_t.append(load_plane("ua3", ua, 3))
+        ub_t.append(load_plane("ub3", ub, 3))
+        l4 = load_list("l4", offs4)
+        l5 = load_list("l5", offs5)
+        l6 = load_list("l6", offs6)
+        ws_w = load_words("ws_w", ws_words)
+        wb_w = load_words("wb_w", wb_words)
+        load_scales(nc.sync, ws_sc, ws_scales)
+        load_scales(nc.sync, wb_sc, wb_scales)
+
+        wc = [tile("wc%d" % u, PACK * P, BF16) for u in range(PACK)]
+
+        def by_r(ap):
+            return ap.rearrange("p (m u) -> p m u", u=PACK)
+
+        last = PACK - 1
+        early = tile("early", last * R, BF16)
+
+        def early_plane(t):
+            ga = tile("ga%d" % t, R, F32)
+            gb = tile("gb%d" % t, R, F32)
+            fetch(ga[:], ua_t[t], l2[:], ha_t, t)
+            fetch(gb[:], ub_t[t], l3[:], hb_t, t)
+            nc.vector.tensor_tensor(
+                out=early[:, t * R:(t + 1) * R].rearrange("p (u m) -> p m u", u=PACK),
+                in0=by_r(ga[:]), in1=by_r(gb[:]), op=MAX,
+            )
+
+        early_plane(0)
+        for q in range(PACK):
+            src = 64 * (q // 2)
+            nc.vector.tensor_copy(
+                out=x_scales[32 * q:32 * q + PACK, :].bitcast(I32), in_=x_stage[src:src + PACK, q % 2, :].bitcast(I32)
+            )
+        xg_scales = tile("xg_scales", J, U8)
+        x7_scales = tile("x7_scales", O, U8)
+        nc.vector.tensor_copy(out=xg_scales[:], in_=x_scales[:].indirect(l1[:]))
+        nc.vector.tensor_copy(out=x7_scales[:], in_=x_scales[:].indirect(l7[:]))
+        early_plane(1)
+        xg_words = tile("xg_words", J, U16)
+        x7_words = tile("x7_words", O, U16)
+        nc.vector.tensor_copy(out=xg_words[:], in_=x_words[:].indirect(l1[:]))
+        early_plane(2)
+        nc.vector.tensor_copy(out=x7_words[:], in_=x_words[:].indirect(l7[:]))
+        for u in range(PACK):
+            nc.vector.tensor_copy(
+                out=wc[u][:].rearrange("p (c i t) -> p c t i", i=PACK, t=PACK)[:, :, :last, :],
+                in_=early[:].rearrange("p (t u c i) -> p u c t i", t=last, u=PACK, i=PACK)[:, u],
+            )
+
+        half = R // 2
+        ga3 = tile("ga3", R, F32)
+        gb3 = tile("gb3", R, F32)
+        fetch(ga3[:], ua_t[3], l2[:], ha_t, 3)
+        fetch(gb3[:, :half], ub_t[3], l3[:, :half // PER_COLUMN], hb_t, 3)
+        m_half = half // PACK
+
+        def last_slot(u):
+            return wc[u][:].rearrange("p (m t) -> p m t", t=PACK)[:, :, last]
+
+        def finish(ms, u):
+            nc.vector.tensor_tensor(
+                out=last_slot(u)[:, ms], in0=by_r(ga3[:])[:, ms, u], in1=by_r(gb3[:])[:, ms, u], op=MAX
+            )
+
+        finish(slice(0, m_half), 0)
+        finish(slice(0, m_half), 1)
+        fetch(gb3[:, half:], ub_t[3], l3[:, half // PER_COLUMN:], hb_t, 3)
+
+        wc_codes = [tile("wc_codes%d" % u, P, U32) for u in range(PACK)]
+        wc_scales = [tile("wc_scales%d" % u, P, U8) for u in range(PACK)]
+
+        def quantise(u):
+            nc.vector.quantize_mx(
+                out=wc_codes[u][:].bitcast(FP8X4), scales=wc_scales[u][:], in_=wc[u][:]
+            )
+
+        finish(slice(m_half, P), 0)
+        finish(slice(m_half, P), 1)
+        quantise(0)
+        quantise(1)
+        late = tile("late", 2 * P, BF16, tag="wc0")
+        nc.vector.tensor_tensor(
+            out=late[:].rearrange("p (u m) -> p m u", u=2), in0=by_r(ga3[:])[:, :, 2:], in1=by_r(gb3[:])[:, :, 2:], op=MAX
+        )
+        for u in range(2, PACK):
+            nc.vector.tensor_copy(out=last_slot(u), in_=late[:, (u - 2) * P:(u - 1) * P])
+        quantise(2)
+        quantise(3)
+
+        a_sb = [tile("a%d" % u, J, F32) for u in range(PACK)]
+
+        def product(u, cols, name):
+            bank = psum.tile([P, cols.stop - cols.start], F32, name=name)
+            nc.tensor.matmul_mx(
+                out=bank[:], lhsT=wc_codes[u][:].bitcast(FP8X4), lhsT_scale=wc_scales[u][:],
+                rhs=xg_words[:, cols].bitcast(FP4X4), rhs_scale=xg_scales[:, cols], start=True, stop=True,
+            )
+            return bank
+
+        for h in range(2):
+            cols = slice(h * J // 2, (h + 1) * J // 2)
+            bank = product(0, cols, "a0_bank%d" % h)
+            nc.scalar.copy(out=a_sb[0][:, cols], in_=bank[:])
+        for u in range(1, PACK):
+            bank = product(u, slice(0, J), "a%d_bank" % u)
+            nc.vector.tensor_copy(out=a_sb[u][:], in_=bank[:])
+
+        y_banks = [psum.tile([P, O], F32, name="y_bank%d" % c) for c in range(N // P)]
+        for c in range(N // P):
+            cols = slice(c * P, (c + 1) * P)
+            nc.tensor.matmul_mx(
+                out=y_banks[c][:], lhsT=ws_w[:, cols].bitcast(FP8X4), lhsT_scale=ws_sc[:, cols],
+                rhs=x7_words[:].bitcast(FP4X4), rhs_scale=x7_scales[:], start=True, stop=False,
+            )
+
+        h1 = [tile("h1_%d" % u, S, F32) for u in range(PACK)]
+        hid = tile("hid", PACK * O, BF16)
+        hid_by_o = hid[:].rearrange("p (o u) -> p o u", u=PACK)
+
+        def places(u):
+            both = tile("g56_%d" % u, 2 * O, F32, tag="a%d" % (u + 1) if u > 0 else None)
+            fetch(both[:, :O], h1[u], l5[:], sb_t, u)
+            fetch(both[:, O:], h1[u], l6[:], sd_t, u)
+            nc.vector.tensor_tensor(out=hid_by_o[:, :, u], in0=both[:, :O], in1=both[:, O:], op=MAX)
+
+        def last_places():
+            g5 = tile("g5_last", O, F32)
+            fetch(g5[:], h1[last], l5[:], sb_t, last)
+            width = O // 2
+            for i in range(2):
+                g6 = tile("g6_last%d" % i, width, F32)
+                cols = slice(i * width, (i + 1) * width)
+                fetch(g6[:], h1[last], l6[:, cols.start // PER_COLUMN:cols.stop // PER_COLUMN], sd_t, last)
+                nc.vector.tensor_tensor(out=hid_by_o[:, cols, last], in0=g5[:, cols], in1=g6[:], op=MAX)
+
+        for u in range(PACK):
+            fetch(h1[u][:], a_sb[u], l4[:], sa_t, u)
+            if u > 0:
+                places(u - 1)
+        last_places()
+        hid_codes = tile("hid_codes", O, U32)
+        hid_scales = tile("hid_scales", O, U8)
+        nc.vector.quantize_mx(out=hid_codes[:].bitcast(FP8X4), scales=hid_scales[:], in_=hid[:])
+
+        for c in range(N // P):
+            cols = slice(c * P, (c + 1) * P)
+            nc.tensor.matmul_mx(
+                out=y_banks[c][:], lhsT=wb_w[:, cols].bitcast(FP8X4), lhsT_scale=wb_sc[:, cols],
+                rhs=hid_codes[:].bitcast(FP8X4), rhs_scale=hid_scales[:], start=False, stop=True,
+            )
+        y0 = tile("y0", O, F32)
+        y1 = tile("y1", O, F32)
+        nc.vector.tensor_copy(out=y0[:], in_=y_banks[0][:])
+        nc.sync.dma_start(out=out[:P, :], in_=y0[:])
+        nc.scalar.copy(out=y1[:], in_=y_banks[1][:])
+        nc.scalar.dma_start(out=out[P:, :], in_=y1[:])

@@ -68,6 +68,10 @@ def tile_picked_tokens_largercode_one_chain_further_plain_kernel(
         x_scales = zeroed_scales("x_scales", T)
         ws_sc = zeroed_scales("ws_sc", N)
         wb_sc = zeroed_scales("wb_sc", N)
+        warm_in = tile("warm_in", 1, F32)
+        warm_out = tile("warm_out", 1, F32)
+        nc.gpsimd.memset(warm_in[:], 0.0)
+        nc.scalar.activation(out=warm_out[:], in_=warm_in[:], func=COPY)
         sa_t = load_factor(nc.gpsimd, "sa_t", sa)
         sb_t = load_factor(nc.gpsimd, "sb_t", sb)
         sd_t = load_factor(nc.gpsimd, "sd_t", sd)

@@ -72,26 +72,28 @@ def tile_picked_tokens_largercode_one_chain_further_plain_kernel(
         warm_out = tile("warm_out", 1, F32)
         nc.gpsimd.memset(warm_in[:], 0.0)
         nc.scalar.activation(out=warm_out[:], in_=warm_in[:], func=COPY)
-        sa_t = load_factor(nc.gpsimd, "sa_t", sa)
-        sb_t = load_factor(nc.gpsimd, "sb_t", sb)
-        sd_t = load_factor(nc.gpsimd, "sd_t", sd)
-
-        ua_t = [load_plane("ua0", ua, 0)]
-        l2 = load_list("l2", offs2)
-        ha_t = load_factor(nc.sync, "ha_t", ha)
-        ub_t = [load_plane("ub0", ub, 0)]
-        l3 = load_list("l3", offs3)
-        hb_t = load_factor(nc.sync, "hb_t", hb)
-        l1 = load_list("l1", offs)
-        ua_t.append(load_plane("ua1", ua, 1))
         x_stage = keep.tile([P, 2, T], U8, name="x_stage", align_bytes=64)
         for h in range(2):
-            nc.sync.dma_start(
+            nc.gpsimd.dma_start(
                 out=x_stage[64 * h:64 * h + PACK].bitcast(I32),
                 in_=xt_scales[0, 8 * h:8 * h + 8, :].rearrange("(q j) c -> j q c", j=PACK).bitcast(I32),
             )
-        l7 = load_list("l7", offs7)
+        for q in range(PACK):
+            src = 64 * (q // 2)
+            nc.vector.tensor_copy(
+                out=x_scales[32 * q:32 * q + PACK, :].bitcast(I32), in_=x_stage[src:src + PACK, q % 2, :].bitcast(I32)
+            )
+        ha_t = load_factor(nc.scalar, "ha_t", ha)
+        hb_t = load_factor(nc.scalar, "hb_t", hb)
+
+        ua_t = [load_plane("ua0", ua, 0)]
+        l2 = load_list("l2", offs2)
+        ub_t = [load_plane("ub0", ub, 0)]
+        l3 = load_list("l3", offs3)
+        ua_t.append(load_plane("ua1", ua, 1))
+        l1 = load_list("l1", offs)
         ub_t.append(load_plane("ub1", ub, 1))
+        l7 = load_list("l7", offs7)
         ua_t.append(load_plane("ua2", ua, 2))
         x_words = tile("x_words", T, U16)
         nc.sync.dma_start(out=x_words[:].bitcast(I32), in_=xt_words[0].bitcast(I32))
@@ -99,20 +101,21 @@ def tile_picked_tokens_largercode_one_chain_further_plain_kernel(
         ua_t.append(load_plane("ua3", ua, 3))
         ub_t.append(load_plane("ub3", ub, 3))
         l4 = load_list("l4", offs4)
+        sa_t = load_factor(nc.sync, "sa_t", sa)
         l5 = load_list("l5", offs5)
+        sb_t = load_factor(nc.sync, "sb_t", sb)
         l6 = load_list("l6", offs6)
+        sd_t = load_factor(nc.sync, "sd_t", sd)
         ws_w = load_words("ws_w", ws_words)
         wb_w = load_words("wb_w", wb_words)
         load_scales(nc.sync, ws_sc, ws_scales)
         load_scales(nc.sync, wb_sc, wb_scales)
 
-        wc = [tile("wc%d" % u, PACK * P, BF16) for u in range(PACK)]
-
         def by_r(ap):
             return ap.rearrange("p (m u) -> p m u", u=PACK)
 
         last = PACK - 1
-        early = tile("early", last * R, BF16)
+        early = tile("early", PACK * R, BF16)
 
         def early_plane(t):
             ga = tile("ga%d" % t, R, F32)
@@ -125,11 +128,6 @@ def tile_picked_tokens_largercode_one_chain_further_plain_kernel(
             )
 
         early_plane(0)
-        for q in range(PACK):
-            src = 64 * (q // 2)
-            nc.vector.tensor_copy(
-                out=x_scales[32 * q:32 * q + PACK, :].bitcast(I32), in_=x_stage[src:src + PACK, q % 2, :].bitcast(I32)
-            )
         xg_scales = tile("xg_scales", J, U8)
         x7_scales = tile("x7_scales", O, U8)
         nc.vector.tensor_copy(out=xg_scales[:], in_=x_scales[:].indirect(l1[:]))
@@ -138,13 +136,20 @@ def tile_picked_tokens_largercode_one_chain_further_plain_kernel(
         xg_words = tile("xg_words", J, U16)
         x7_words = tile("x7_words", O, U16)
         nc.vector.tensor_copy(out=xg_words[:], in_=x_words[:].indirect(l1[:]))
-        early_plane(2)
         nc.vector.tensor_copy(out=x7_words[:], in_=x_words[:].indirect(l7[:]))
-        for u in range(PACK):
+        early_plane(2)
+
+        wc = []
+
+        def weave(u, planes):
+            wc.append(tile("wc%d" % u, PACK * P, BF16, tag="wc%d" % (u % 2)))
             nc.vector.tensor_copy(
-                out=wc[u][:].rearrange("p (c i t) -> p c t i", i=PACK, t=PACK)[:, :, :last, :],
-                in_=early[:].rearrange("p (t u c i) -> p u c t i", t=last, u=PACK, i=PACK)[:, u],
+                out=wc[u][:].rearrange("p (c i t) -> p c t i", i=PACK, t=PACK)[:, :, :planes, :],
+                in_=early[:].rearrange("p (t u c i) -> p u c t i", t=PACK, u=PACK, i=PACK)[:, u, :, :planes, :],
             )
+
+        weave(0, last)
+        weave(1, last)
 
         half = R // 2
         ga3 = tile("ga3", R, F32)
@@ -174,15 +179,15 @@ def tile_picked_tokens_largercode_one_chain_further_plain_kernel(
             )
 
         finish(slice(m_half, P), 0)
-        finish(slice(m_half, P), 1)
-        quantise(0)
-        quantise(1)
-        late = tile("late", 2 * P, BF16, tag="wc0")
         nc.vector.tensor_tensor(
-            out=late[:].rearrange("p (u m) -> p m u", u=2), in0=by_r(ga3[:])[:, :, 2:], in1=by_r(gb3[:])[:, :, 2:], op=MAX
+            out=early[:, last * R:].rearrange("p (u m) -> p m u", u=PACK)[:, :, 2:],
+            in0=by_r(ga3[:])[:, :, 2:], in1=by_r(gb3[:])[:, :, 2:], op=MAX,
         )
-        for u in range(2, PACK):
-            nc.vector.tensor_copy(out=last_slot(u), in_=late[:, (u - 2) * P:(u - 1) * P])
+        quantise(0)
+        finish(slice(m_half, P), 1)
+        weave(2, PACK)
+        quantise(1)
+        weave(3, PACK)
         quantise(2)
         quantise(3)
 
@@ -196,9 +201,8 @@ def tile_picked_tokens_largercode_one_chain_further_plain_kernel(
             )
             return bank
 
-        for h in range(2):
-            cols = slice(h * J // 2, (h + 1) * J // 2)
-            bank = product(0, cols, "a0_bank%d" % h)
+        for cols in (slice(0, 256), slice(256, 384), slice(384, 512)):
+            bank = product(0, cols, "a0_bank%d" % cols.start)
             nc.scalar.copy(out=a_sb[0][:, cols], in_=bank[:])
         for u in range(1, PACK):
             bank = product(u, slice(0, J), "a%d_bank" % u)

@@ -93,13 +93,13 @@ def tile_picked_tokens_largercode_one_chain_further_plain_kernel(
         ua_t.append(load_plane("ua1", ua, 1))
         l1 = load_list("l1", offs)
         ub_t.append(load_plane("ub1", ub, 1))
-        l7 = load_list("l7", offs7)
         ua_t.append(load_plane("ua2", ua, 2))
         x_words = tile("x_words", T, U16)
         nc.sync.dma_start(out=x_words[:].bitcast(I32), in_=xt_words[0].bitcast(I32))
         ub_t.append(load_plane("ub2", ub, 2))
         ua_t.append(load_plane("ua3", ua, 3))
         ub_t.append(load_plane("ub3", ub, 3))
+        l7 = load_list("l7", offs7)
         l4 = load_list("l4", offs4)
         sa_t = load_factor(nc.sync, "sa_t", sa)
         l5 = load_list("l5", offs5)
@@ -131,12 +131,10 @@ def tile_picked_tokens_largercode_one_chain_further_plain_kernel(
         xg_scales = tile("xg_scales", J, U8)
         x7_scales = tile("x7_scales", O, U8)
         nc.vector.tensor_copy(out=xg_scales[:], in_=x_scales[:].indirect(l1[:]))
-        nc.vector.tensor_copy(out=x7_scales[:], in_=x_scales[:].indirect(l7[:]))
         early_plane(1)
         xg_words = tile("xg_words", J, U16)
         x7_words = tile("x7_words", O, U16)
         nc.vector.tensor_copy(out=xg_words[:], in_=x_words[:].indirect(l1[:]))
-        nc.vector.tensor_copy(out=x7_words[:], in_=x_words[:].indirect(l7[:]))
         early_plane(2)
 
         wc = []
@@ -150,6 +148,8 @@ def tile_picked_tokens_largercode_one_chain_further_plain_kernel(
 
         weave(0, last)
         weave(1, last)
+        nc.vector.tensor_copy(out=x7_scales[:], in_=x_scales[:].indirect(l7[:]))
+        nc.vector.tensor_copy(out=x7_words[:], in_=x_words[:].indirect(l7[:]))
 
         half = R // 2
         ga3 = tile("ga3", R, F32)
@@ -201,7 +201,7 @@ def tile_picked_tokens_largercode_one_chain_further_plain_kernel(
             )
             return bank
 
-        for cols in (slice(0, 256), slice(256, 384), slice(384, 512)):
+        for cols in (slice(0, J // 2), slice(J // 2, J)):
             bank = product(0, cols, "a0_bank%d" % cols.start)
             nc.scalar.copy(out=a_sb[0][:, cols], in_=bank[:])
         for u in range(1, PACK):

from contextlib import ExitStack

import concourse.mybir as mybir

K, J, R, T, F, G, O, S, N = 512, 512, 512, 1024, 1024, 1024, 128, 256, 256
FLOPS = 2 * K * R * J + 2 * R * N * O + 2 * K * N * O

F32 = mybir.dt.float32
BF16 = mybir.dt.bfloat16
I32 = mybir.dt.int32
U32 = mybir.dt.uint32
U16 = mybir.dt.uint16
U8 = mybir.dt.uint8
FP8X4 = mybir.dt.float8_e4m3fn_x4
FP4X4 = mybir.dt.float4_e2m1fn_x4
COPY = mybir.ActivationFunctionType.Copy
MAX = mybir.AluOpType.max

P = 128
PACK = 4
PER_COLUMN = 16


def tile_picked_tokens_largercode_one_chain_further_plain_kernel(
    tc, xt_words, xt_scales, ua, ub, ha, hb, sa, sb, sd, wb_words, wb_scales, ws_words, ws_scales,
    offs, offs2, offs3, offs4, offs5, offs6, offs7, out,
):
    nc = tc.nc
    with ExitStack() as ctx:
        keep = ctx.enter_context(tc.tile_pool(name="keep", bufs=1))
        psum = ctx.enter_context(tc.psum_pool(name="psum", bufs=1))

        def tile(name, columns, dtype, tag=None):
            return keep.tile([P, columns], dtype, name=name, tag=tag or name, align_bytes=64)

        def load_list(name, source):
            held = tile(name, source.shape[1], U16)
            nc.sync.dma_start(held[:], source)
            return held

        def load_factor(queue, name, source):
            held = tile(name, PACK, F32)
            queue.dma_start(out=held[:], in_=source.rearrange("(p t) one -> p (t one)", t=PACK))
            return held

        def load_plane(name, table, t):
            held = tile(name, table.shape[1], F32)
            nc.sync.dma_start(out=held[:], in_=table.rearrange("(p t) f -> p t f", t=PACK)[:, t, :])
            return held

        def zeroed_scales(name, columns):
            held = tile(name, columns, U8)
            nc.vector.memset(held[:].bitcast(I32), 0)
            return held

        def load_scales(queue, held, source):
            for row in range(PACK):
                queue.dma_start(out=held[row:P:32, :].bitcast(I32), in_=source[0, row:16:PACK, :].bitcast(I32))

        def load_words(name, source):
            held = tile(name, N, U32)
            nc.sync.dma_start(out=held[:].bitcast(I32), in_=source[0].rearrange("p n t -> p (n t)").bitcast(I32))
            return held

        def fetch(dst, window, offsets, factor, t):
            nc.scalar.activation(out=dst, in_=window[:].indirect(offsets), func=COPY, scale=factor[:, t:t + 1])

        x_scales = zeroed_scales("x_scales", T)
        ws_sc = zeroed_scales("ws_sc", N)
        wb_sc = zeroed_scales("wb_sc", N)
        warm_in = tile("warm_in", 1, F32)
        warm_out = tile("warm_out", 1, F32)
        nc.gpsimd.memset(warm_in[:], 0.0)
        nc.scalar.activation(out=warm_out[:], in_=warm_in[:], func=COPY)
        x_stage = keep.tile([P, 2, T], U8, name="x_stage", align_bytes=64)
        for h in range(2):
            nc.gpsimd.dma_start(
                out=x_stage[64 * h:64 * h + PACK].bitcast(I32),
                in_=xt_scales[0, 8 * h:8 * h + 8, :].rearrange("(q j) c -> j q c", j=PACK).bitcast(I32),
            )
        for q in range(PACK):
            src = 64 * (q // 2)
            nc.vector.tensor_copy(
                out=x_scales[32 * q:32 * q + PACK, :].bitcast(I32), in_=x_stage[src:src + PACK, q % 2, :].bitcast(I32)
            )
        ha_t = load_factor(nc.scalar, "ha_t", ha)
        hb_t = load_factor(nc.scalar, "hb_t", hb)

        ua_t = [load_plane("ua0", ua, 0)]
        l2 = load_list("l2", offs2)
        ub_t = [load_plane("ub0", ub, 0)]
        l3 = load_list("l3", offs3)
        ua_t.append(load_plane("ua1", ua, 1))
        l1 = load_list("l1", offs)
        ub_t.append(load_plane("ub1", ub, 1))
        ua_t.append(load_plane("ua2", ua, 2))
        x_words = tile("x_words", T, U16)
        nc.sync.dma_start(out=x_words[:].bitcast(I32), in_=xt_words[0].bitcast(I32))
        ub_t.append(load_plane("ub2", ub, 2))
        ua_t.append(load_plane("ua3", ua, 3))
        ub_t.append(load_plane("ub3", ub, 3))
        l7 = load_list("l7", offs7)
        l4 = load_list("l4", offs4)
        sa_t = load_factor(nc.sync, "sa_t", sa)
        l5 = load_list("l5", offs5)
        sb_t = load_factor(nc.sync, "sb_t", sb)
        l6 = load_list("l6", offs6)
        sd_t = load_factor(nc.sync, "sd_t", sd)
        ws_w = load_words("ws_w", ws_words)
        wb_w = load_words("wb_w", wb_words)
        load_scales(nc.sync, ws_sc, ws_scales)
        load_scales(nc.sync, wb_sc, wb_scales)

        def by_r(ap):
            return ap.rearrange("p (m u) -> p m u", u=PACK)

        last = PACK - 1
        early = tile("early", PACK * R, BF16)

        def early_plane(t):
            ga = tile("ga%d" % t, R, F32)
            gb = tile("gb%d" % t, R, F32)
            fetch(ga[:], ua_t[t], l2[:], ha_t, t)
            fetch(gb[:], ub_t[t], l3[:], hb_t, t)
            nc.vector.tensor_tensor(
                out=early[:, t * R:(t + 1) * R].rearrange("p (u m) -> p m u", u=PACK),
                in0=by_r(ga[:]), in1=by_r(gb[:]), op=MAX,
            )

        early_plane(0)
        xg_scales = tile("xg_scales", J, U8)
        x7_scales = tile("x7_scales", O, U8)
        nc.vector.tensor_copy(out=xg_scales[:], in_=x_scales[:].indirect(l1[:]))
        early_plane(1)
        xg_words = tile("xg_words", J, U16)
        x7_words = tile("x7_words", O, U16)
        nc.vector.tensor_copy(out=xg_words[:], in_=x_words[:].indirect(l1[:]))
        early_plane(2)

        wc = []

        def weave(u, planes):
            wc.append(tile("wc%d" % u, PACK * P, BF16, tag="wc%d" % (u % 2)))
            nc.vector.tensor_copy(
                out=wc[u][:].rearrange("p (c i t) -> p c t i", i=PACK, t=PACK)[:, :, :planes, :],
                in_=early[:].rearrange("p (t u c i) -> p u c t i", t=PACK, u=PACK, i=PACK)[:, u, :, :planes, :],
            )

        weave(0, last)
        weave(1, last)
        nc.vector.tensor_copy(out=x7_scales[:], in_=x_scales[:].indirect(l7[:]))
        nc.vector.tensor_copy(out=x7_words[:], in_=x_words[:].indirect(l7[:]))

        half = R // 2
        ga3 = tile("ga3", R, F32)
        gb3 = tile("gb3", R, F32)
        fetch(ga3[:], ua_t[3], l2[:], ha_t, 3)
        fetch(gb3[:, :half], ub_t[3], l3[:, :half // PER_COLUMN], hb_t, 3)
        m_half = half // PACK

        def last_slot(u):
            return wc[u][:].rearrange("p (m t) -> p m t", t=PACK)[:, :, last]

        def finish(ms, u):
            nc.vector.tensor_tensor(
                out=last_slot(u)[:, ms], in0=by_r(ga3[:])[:, ms, u], in1=by_r(gb3[:])[:, ms, u], op=MAX
            )

        finish(slice(0, m_half), 0)
        finish(slice(0, m_half), 1)
        fetch(gb3[:, half:], ub_t[3], l3[:, half // PER_COLUMN:], hb_t, 3)

        wc_codes = [tile("wc_codes%d" % u, P, U32) for u in range(PACK)]
        wc_scales = [tile("wc_scales%d" % u, P, U8) for u in range(PACK)]

        def quantise(u):
            nc.vector.quantize_mx(
                out=wc_codes[u][:].bitcast(FP8X4), scales=wc_scales[u][:], in_=wc[u][:]
            )

        finish(slice(m_half, P), 0)
        nc.vector.tensor_tensor(
            out=early[:, last * R:].rearrange("p (u m) -> p m u", u=PACK)[:, :, 2:],
            in0=by_r(ga3[:])[:, :, 2:], in1=by_r(gb3[:])[:, :, 2:], op=MAX,
        )
        quantise(0)
        finish(slice(m_half, P), 1)
        weave(2, PACK)
        quantise(1)
        weave(3, PACK)
        quantise(2)
        quantise(3)

        a_sb = [tile("a%d" % u, J, F32) for u in range(PACK)]

        def product(u, cols, name):
            bank = psum.tile([P, cols.stop - cols.start], F32, name=name)
            nc.tensor.matmul_mx(
                out=bank[:], lhsT=wc_codes[u][:].bitcast(FP8X4), lhsT_scale=wc_scales[u][:],
                rhs=xg_words[:, cols].bitcast(FP4X4), rhs_scale=xg_scales[:, cols], start=True, stop=True,
            )
            return bank

        for cols in (slice(0, J // 2), slice(J // 2, J)):
            bank = product(0, cols, "a0_bank%d" % cols.start)
            nc.scalar.copy(out=a_sb[0][:, cols], in_=bank[:])
        for u in range(1, PACK):
            bank = product(u, slice(0, J), "a%d_bank" % u)
            nc.vector.tensor_copy(out=a_sb[u][:], in_=bank[:])

        y_banks = [psum.tile([P, O], F32, name="y_bank%d" % c) for c in range(N // P)]
        for c in range(N // P):
            cols = slice(c * P, (c + 1) * P)
            nc.tensor.matmul_mx(
                out=y_banks[c][:], lhsT=ws_w[:, cols].bitcast(FP8X4), lhsT_scale=ws_sc[:, cols],
                rhs=x7_words[:].bitcast(FP4X4), rhs_scale=x7_scales[:], start=True, stop=False,
            )

        h1 = [tile("h1_%d" % u, S, F32) for u in range(PACK)]
        hid = tile("hid", PACK * O, BF16)
        hid_by_o = hid[:].rearrange("p (o u) -> p o u", u=PACK)

        def places(u):
            both = tile("g56_%d" % u, 2 * O, F32, tag="a%d" % (u + 1) if u > 0 else None)
            fetch(both[:, :O], h1[u], l5[:], sb_t, u)
            fetch(both[:, O:], h1[u], l6[:], sd_t, u)
            nc.vector.tensor_tensor(out=hid_by_o[:, :, u], in0=both[:, :O], in1=both[:, O:], op=MAX)

        def last_places():
            g5 = tile("g5_last", O, F32)
            fetch(g5[:], h1[last], l5[:], sb_t, last)
            width = O // 2
            for i in range(2):
                g6 = tile("g6_last%d" % i, width, F32)
                cols = slice(i * width, (i + 1) * width)
                fetch(g6[:], h1[last], l6[:, cols.start // PER_COLUMN:cols.stop // PER_COLUMN], sd_t, last)
                nc.vector.tensor_tensor(out=hid_by_o[:, cols, last], in0=g5[:, cols], in1=g6[:], op=MAX)

        for u in range(PACK):
            fetch(h1[u][:], a_sb[u], l4[:], sa_t, u)
            if u > 0:
                places(u - 1)
        last_places()
        hid_codes = tile("hid_codes", O, U32)
        hid_scales = tile("hid_scales", O, U8)
        nc.vector.quantize_mx(out=hid_codes[:].bitcast(FP8X4), scales=hid_scales[:], in_=hid[:])

        for c in range(N // P):
            cols = slice(c * P, (c + 1) * P)
            nc.tensor.matmul_mx(
                out=y_banks[c][:], lhsT=wb_w[:, cols].bitcast(FP8X4), lhsT_scale=wb_sc[:, cols],
                rhs=hid_codes[:].bitcast(FP8X4), rhs_scale=hid_scales[:], start=False, stop=True,
            )
        y0 = tile("y0", O, F32)
        y1 = tile("y1", O, F32)
        nc.vector.tensor_copy(out=y0[:], in_=y_banks[0][:])
        nc.sync.dma_start(out=out[:P, :], in_=y0[:])
        nc.scalar.copy(out=y1[:], in_=y_banks[1][:])
        nc.scalar.dma_start(out=out[P:, :], in_=y1[:])
